import numpy as np
import ml_dtypes


def mxq(x, axis, fmt="e4m3"):
    dtype, down = {"e4m3": (ml_dtypes.float8_e4m3fn, 7), "e5m2": (ml_dtypes.float8_e5m2, 14)}[fmt]
    v = np.moveaxis(np.asarray(x, np.float32).astype(ml_dtypes.bfloat16).astype(np.float64), axis, -1)
    blocks = v.reshape(v.shape[:-1] + (-1, 32))
    amax = np.abs(blocks).max(-1, keepdims=True)
    byte = np.maximum(np.where(amax > 0, np.frexp(amax)[1] - 1 + 127, 0) - down, 1)
    scale = np.exp2(byte - 127.0)
    codes = (blocks / scale).astype(np.float32).astype(dtype).astype(np.float64)
    return np.moveaxis((codes * scale).reshape(v.shape), -1, axis)


WIDE = False


def mx_kscale(k):
    if not WIDE:
        return np.ones(k)
    levels = np.array([30, -30])
    if k % 512:
        return np.exp2(np.random.permutation(np.resize(levels, k // 32))).repeat(32)
    a = np.empty((k // 512, 16))
    for p in range(k // 512):
        a[p, :8] = np.random.permutation(np.resize(levels, 8))
        for g in range(8):
            far = levels[np.abs(levels - a[p, g]) >= 10]
            a[p, g + 8] = far[np.random.randint(len(far))]
    return np.exp2(a.ravel()).repeat(32)


def f64(x):
    return np.asarray(x).astype(np.float64)


def striped(idx):
    return np.tile(np.asarray(idx).reshape(-1, 16).T, (8, 1)).astype(np.uint16)


def unstriped(offs):
    return offs[:16].T.reshape(-1).astype(np.int64)


def striped8(idx):
    return np.asarray(idx).reshape(8, -1, 16).transpose(0, 2, 1).reshape(128, -1).astype(np.uint16)


def unstriped8(offs):
    return offs.reshape(8, 16, -1).transpose(0, 2, 1).reshape(8, -1).astype(np.int64)


def pick8(x, idx, run):
    r = np.arange(len(x))
    return x[r[:, None], idx[r % (8 * run) // run]]


E2M1 = np.array([0.0, 0.5, 1.0, 1.5, 2.0, 3.0, 4.0, 6.0, -0.0, -0.5, -1.0, -1.5, -2.0, -3.0, -4.0, -6.0])


def pack_weight(w, fmt):
    k, n = w.shape
    w = f64(np.asarray(w, np.float32).astype(ml_dtypes.bfloat16)).reshape(k // 32, 32, n)
    amax = np.abs(w).max(1)
    if fmt == "e4m3":
        byte = np.frexp(amax)[1] - 1 + 127 - 7
    else:
        mant, ex = np.frexp(amax / 6.0)
        byte = np.where(mant > 0.5, ex, ex - 1) + 127
    byte = np.clip(np.where(amax > 0, byte, 1), 1, 254)
    scaled = (w * np.exp2(127.0 - byte)[:, None, :]).reshape(k, n).astype(np.float32)
    by_word = np.ascontiguousarray(scaled.reshape(k // 512, 128, 4, n).transpose(0, 1, 3, 2))
    if fmt == "e4m3":
        words = by_word.astype(ml_dtypes.float8_e4m3fn).view(np.uint8)
    else:
        c = by_word.astype(ml_dtypes.float4_e2m1fn).view(np.uint8) & 0xF
        words = (c[..., 0::2] | (c[..., 1::2] << 4)).reshape(k // 512, 128, 2 * n)
    return np.ascontiguousarray(words), np.ascontiguousarray(byte.astype(np.uint8).reshape(k // 512, 16, n))


def unpack_weight(words, scales, fmt):
    g, _, n = scales.shape
    words = np.ascontiguousarray(words).reshape(g, 128, n, -1)
    if fmt == "e4m3":
        vals = words.view(ml_dtypes.float8_e4m3fn).astype(np.float64)
    else:
        nib = np.empty((g, 128, n, 4), np.uint8)
        nib[..., 0::2] = words & 0xF
        nib[..., 1::2] = words >> 4
        vals = E2M1[nib]
    vals = vals * np.repeat(np.exp2(scales.astype(np.float64) - 127.0), 8, axis=1)[..., None]
    return vals.transpose(0, 1, 3, 2).reshape(g * 512, n)


K, T, J, R, V, N = 1024, 512, 128, 512, 512, 256


def setup_inputs():
    n = np.random.standard_normal
    idx = np.stack([np.random.permutation(T)[:J] for _ in range(8)])
    idx2 = np.random.permutation(V)[:J]
    fk = mx_kscale(K)
    fr = mx_kscale(R)
    xtp = pack_weight(n((K, T)) / fk[:, None], "e4m3")
    wbp = pack_weight(n((R, N)) * 1 / np.sqrt(R) / fr[:, None], "e2m1")
    return {
        "xt_words": xtp[0],
        "xt_scales": xtp[1],
        "w": (n((K, R)) * 1 / np.sqrt(K) * fk[:, None] * fr).astype(np.float32),
        "tb": (n((R, V)) * 0.7 * fr[:, None]).astype(np.float32),
        "wb_words": wbp[0],
        "wb_scales": wbp[1],
        "rs": (1.0 * n((J, N))).astype(np.float32),
        "offs": striped8(idx),
        "offs2": striped(idx2),
    }


def reference(xt_words, xt_scales, w, tb, wb_words, wb_scales, rs, offs, offs2):
    idx = unstriped8(offs)
    idx2 = unstriped(offs2)
    xtu = unpack_weight(xt_words, xt_scales, "e4m3")
    wbu = unpack_weight(wb_words, wb_scales, "e2m1")
    wq = mxq(f64(w), 0, "e5m2")
    xtidxg = pick8(xtu, idx, 64)
    a = wq.T @ xtidxg
    hid = np.maximum(a - f64(tb)[:, idx2], 0.0)
    hidq = mxq(hid, 0, "e5m2")
    p = hidq.T @ wbu
    mn = np.mean(np.abs(p), axis=1, keepdims=True)
    y = np.maximum(p - mn, 0.0) - 0.3 * f64(rs)
    return y

@@ -1,0 +1,168 @@
+from contextlib import ExitStack
+
+import concourse.mybir as mybir
+
+F32 = mybir.dt.float32
+BF16 = mybir.dt.bfloat16
+I32 = mybir.dt.int32
+U32 = mybir.dt.uint32
+U16 = mybir.dt.uint16
+U8 = mybir.dt.uint8
+E4M3X4 = mybir.dt.float8_e4m3fn_x4
+E5M2X4 = mybir.dt.float8_e5m2_x4
+E2M1X4 = mybir.dt.float4_e2m1fn_x4
+ALU = mybir.AluOpType
+ACT = mybir.ActivationFunctionType
+
+P = 128
+PACK = 4
+K, T, J, R, V, N = 1024, 512, 128, 512, 512, 256
+PASSES = K // (P * PACK)
+QUADS = 4
+VECTOR_ROWS = 80
+FLOPS = 2 * K * R * J + 2 * R * J * N
+
+
+def tile_list_headpicks_overtable_rowabove_kernel(tc, xt_words, xt_scales, w, tb, wb_words, wb_scales, rs, offs, offs2, out):
+    nc = tc.nc
+    with ExitStack() as ctx:
+        sb = ctx.enter_context(tc.tile_pool(name="sb", bufs=1))
+        reused = ctx.enter_context(tc.tile_pool(name="reused", bufs=1))
+        ps = ctx.enter_context(tc.psum_pool(name="ps", bufs=1))
+
+        heads_list = sb.tile([P, J // 16], U16, name="heads_list")
+        table_list = sb.tile([P, J // 16], U16, name="table_list")
+        xs_picked = sb.tile([P, J], U8, name="xs_picked", align_bytes=64)
+        x_scales = sb.tile([P, PASSES * J], U8, name="x_scales", align_bytes=64)
+        wb_plane = sb.tile([P, N], U8, name="wb_plane", align_bytes=64)
+        w_bytes = PACK * R * 4
+        w_raw = [
+            reused.tile([P, PACK, R], F32, name="w_raw%d" % z, align_bytes=64, offset=z * w_bytes) for z in range(PASSES)
+        ]
+        bf_at = PASSES * w_bytes
+        xs_window = reused.tile([P, T], U8, name="xs_window", align_bytes=64, offset=bf_at + VECTOR_ROWS * 8 - 256)
+        xw_window = [sb.tile([P, T], U32, name="xw_window%d" % z, align_bytes=64) for z in range(PASSES)]
+
+        nc.vector.memset(xs_window[:].bitcast(I32), 0)
+        nc.gpsimd.memset(x_scales[:].bitcast(I32), 0)
+        nc.gpsimd.memset(wb_plane[:].bitcast(I32), 0)
+
+        nc.sync.dma_start(heads_list[:], offs)
+        nc.scalar.dma_start(
+            xs_window[:].bitcast(I32)[0:P:4, :],
+            xt_scales.rearrange("z q c -> q z c").bitcast(I32),
+        )
+        w_rows = w.rearrange("(z p j) r -> z p j r", z=PASSES, j=PACK)
+        nc.sync.dma_start(w_raw[0][:], w_rows[0])
+        nc.sync.dma_start(table_list[:], offs2)
+        x_rows = xt_words.rearrange("z p c b -> z p (c b)").bitcast(I32)
+        nc.sync.dma_start(xw_window[0][:].bitcast(I32), x_rows[0])
+        nc.sync.dma_start(w_raw[1][:], w_rows[1])
+        nc.sync.dma_start(xw_window[1][:].bitcast(I32), x_rows[1])
+        for q in range(QUADS):
+            nc.gpsimd.dma_start(
+                wb_plane[:].bitcast(I32)[32 * q : 32 * q + 4, :],
+                wb_scales[0, 4 * q : 4 * q + 4, :].bitcast(I32),
+            )
+
+        nc.vector.tensor_copy(xs_picked[:], xs_window[:].indirect(heads_list[:]))
+        for q in range(QUADS):
+            nc.scalar.dma_start(
+                x_scales[:].bitcast(I32)[32 * q : 32 * q + 4, :],
+                xs_picked[:].bitcast(I32)[32 * q : 32 * q + 32 : 4, :],
+            )
+
+        w_codes, w_scales = [], []
+        for z in range(PASSES):
+            w_bf = reused.tile([P, PACK, P, PACK], BF16, name="w_bf%d" % z, align_bytes=64, offset=bf_at + z * w_bytes // 2)
+            src = w_raw[z][:].rearrange("p j (m t) -> p m j t", t=PACK)
+            dst = w_bf[:].rearrange("p t m j -> p m j t")
+            nc.vector.tensor_copy(dst[:, :VECTOR_ROWS], src[:, :VECTOR_ROWS])
+            nc.scalar.activation(dst[:, VECTOR_ROWS:], src[:, VECTOR_ROWS:], ACT.Copy)
+            codes = sb.tile([P, R], U32, name="w_codes%d" % z, align_bytes=64)
+            scales = sb.tile([P, R], U8, name="w_scales%d" % z, align_bytes=64)
+            flat = w_bf[:].rearrange("p t m j -> p (t m j)")
+            for half in range(2):
+                nc.vector.quantize_mx(
+                    out=codes[:, 256 * half : 256 * (half + 1)].bitcast(E5M2X4),
+                    scales=scales[:, 256 * half : 256 * (half + 1)],
+                    in_=flat[:, 1024 * half : 1024 * (half + 1)],
+                )
+            w_codes.append(codes)
+            w_scales.append(scales)
+
+        tb_rows = tb.rearrange("(p t) v -> p t v", t=PACK)
+        tb_pair = reused.tile([P, 2, V], F32, name="tb_pair", align_bytes=64, offset=0)
+        nc.sync.dma_start(tb_pair[:], tb_rows[:, 0:2, :])
+        tb_window = [tb_pair[:, 0, :], tb_pair[:, 1, :]]
+        for t in range(2, PACK):
+            tb_single = reused.tile([P, V], F32, name="tb_single%d" % t, align_bytes=64, offset=t * V * 4)
+            nc.sync.dma_start(tb_single[:], tb_rows[:, t, :])
+            tb_window.append(tb_single[:])
+        wb_codes = reused.tile([P, 2 * N], U8, name="wb_codes", align_bytes=64, offset=w_bytes)
+        nc.sync.dma_start(wb_codes[:].bitcast(I32), wb_words[0].bitcast(I32))
+        rs_sb = reused.tile([P, N], F32, name="rs_sb", align_bytes=64, offset=w_bytes + 2 * N)
+        nc.sync.dma_start(rs_sb[:], rs)
+
+        x_codes = []
+        for z in range(PASSES):
+            picked = sb.tile([P, J], U32, name="x_codes%d" % z, align_bytes=64)
+            nc.vector.tensor_copy(picked[:], xw_window[z][:].indirect(heads_list[:]))
+            x_codes.append(picked)
+
+        acc = [ps.tile([P, J], F32, name="acc%d" % t) for t in range(PACK)]
+        for z in range(PASSES):
+            for t in range(PACK):
+                nc.tensor.matmul_mx(
+                    out=acc[t][:],
+                    lhsT=w_codes[z][:, P * t : P * (t + 1)].bitcast(E5M2X4),
+                    lhsT_scale=w_scales[z][:, P * t : P * (t + 1)],
+                    rhs=x_codes[z][:].bitcast(E4M3X4),
+                    rhs_scale=x_scales[:, J * z : J * (z + 1)],
+                    start=(z == 0),
+                    stop=(z == PASSES - 1),
+                )
+
+        gap = sb.tile([P, PACK, J], F32, name="gap", align_bytes=64)
+        for t in range(2):
+            tb_picked = sb.tile([P, J], F32, name="tb_picked%d" % t, align_bytes=64)
+            nc.scalar.activation(tb_picked[:], tb_window[t].indirect(table_list[:]), ACT.Copy)
+            nc.vector.tensor_tensor(gap[:, t, :], tb_picked[:], acc[t][:], ALU.subtract)
+        for t in range(2, PACK):
+            a_sb = sb.tile([P, J], F32, name="a_sb%d" % t, align_bytes=64)
+            nc.scalar.copy(a_sb[:], acc[t][:])
+            nc.vector.tensor_tensor(gap[:, t, :], tb_window[t].indirect(table_list[:]), a_sb[:], ALU.subtract)
+
+        hid = sb.tile([P, J, PACK], BF16, name="hid", align_bytes=64)
+        nc.vector.tensor_scalar(
+            hid[:].rearrange("p (c i) t -> p c t i", i=4),
+            gap[:].rearrange("p t (c i) -> p c t i", i=4),
+            -1.0, 0.0, ALU.mult, ALU.max,
+        )
+        h_codes = sb.tile([P, J], U32, name="h_codes", align_bytes=64)
+        h_scales = sb.tile([P, J], U8, name="h_scales", align_bytes=64)
+        nc.vector.quantize_mx(
+            out=h_codes[:].bitcast(E5M2X4), scales=h_scales[:], in_=hid[:].rearrange("p j t -> p (j t)")
+        )
+
+        prod = ps.tile([P, N], F32, name="prod")
+        nc.tensor.matmul_mx(
+            out=prod[:],
+            lhsT=h_codes[:].bitcast(E5M2X4),
+            lhsT_scale=h_scales[:],
+            rhs=wb_codes[:].bitcast(E2M1X4),
+            rhs_scale=wb_plane[:],
+            start=True,
+            stop=True,
+        )
+
+        minus_rs = sb.tile([P, N], F32, name="minus_rs", align_bytes=64)
+        nc.scalar.activation(minus_rs[:], rs_sb[:], ACT.Copy, scale=-0.3)
+        shifted = sb.tile([P, N], F32, name="shifted", align_bytes=64)
+        nc.vector.tensor_tensor(shifted[:], prod[:], minus_rs[:], ALU.add)
+        magnitude = sb.tile([P, N], F32, name="magnitude", align_bytes=64)
+        mean = sb.tile([P, 1], F32, name="mean", align_bytes=64)
+        nc.scalar.activation(magnitude[:], prod[:], ACT.Abs, scale=1.0 / N, accum_out=mean[:])
+        result = sb.tile([P, N], F32, name="result", align_bytes=64)
+        nc.vector.scalar_tensor_tensor(result[:], shifted[:], mean[:], minus_rs[:], ALU.subtract, ALU.max)
+        nc.sync.dma_start(out, result[:])

@@ -19,7 +19,7 @@ PACK = 4
 K, T, J, R, V, N = 1024, 512, 128, 512, 512, 256
 PASSES = K // (P * PACK)
 QUADS = 4
-VECTOR_ROWS = 80
+VECTOR_ROWS = (84, 64)
 FLOPS = 2 * K * R * J + 2 * R * J * N
 
 
@@ -40,7 +40,7 @@ def tile_list_headpicks_overtable_rowabove_kernel(tc, xt_words, xt_scales, w, tb
             reused.tile([P, PACK, R], F32, name="w_raw%d" % z, align_bytes=64, offset=z * w_bytes) for z in range(PASSES)
         ]
         bf_at = PASSES * w_bytes
-        xs_window = reused.tile([P, T], U8, name="xs_window", align_bytes=64, offset=bf_at + VECTOR_ROWS * 8 - 256)
+        xs_window = reused.tile([P, T], U8, name="xs_window", align_bytes=64, offset=bf_at + w_bytes - 256)
         xw_window = [sb.tile([P, T], U32, name="xw_window%d" % z, align_bytes=64) for z in range(PASSES)]
 
         nc.vector.memset(xs_window[:].bitcast(I32), 0)
@@ -55,9 +55,11 @@ def tile_list_headpicks_overtable_rowabove_kernel(tc, xt_words, xt_scales, w, tb
         w_rows = w.rearrange("(z p j) r -> z p j r", z=PASSES, j=PACK)
         nc.sync.dma_start(w_raw[0][:], w_rows[0])
         nc.sync.dma_start(table_list[:], offs2)
+        wb_codes = sb.tile([P, 2 * N], U8, name="wb_codes", align_bytes=64)
+        nc.sync.dma_start(wb_codes[:].bitcast(I32), wb_words[0].bitcast(I32))
         x_rows = xt_words.rearrange("z p c b -> z p (c b)").bitcast(I32)
-        nc.sync.dma_start(xw_window[0][:].bitcast(I32), x_rows[0])
         nc.sync.dma_start(w_raw[1][:], w_rows[1])
+        nc.sync.dma_start(xw_window[0][:].bitcast(I32), x_rows[0])
         nc.sync.dma_start(xw_window[1][:].bitcast(I32), x_rows[1])
         for q in range(QUADS):
             nc.gpsimd.dma_start(
@@ -65,20 +67,31 @@ def tile_list_headpicks_overtable_rowabove_kernel(tc, xt_words, xt_scales, w, tb
                 wb_scales[0, 4 * q : 4 * q + 4, :].bitcast(I32),
             )
 
+        warm_in = sb.tile([P, 1], F32, name="warm_in")
+        warm_out = sb.tile([P, 1], F32, name="warm_out")
+        nc.vector.memset(warm_in[:], 0.0)
+        nc.scalar.activation(warm_out[:], warm_in[:], ACT.Abs)
+
         nc.vector.tensor_copy(xs_picked[:], xs_window[:].indirect(heads_list[:]))
         for q in range(QUADS):
-            nc.scalar.dma_start(
+            nc.sync.dma_start(
                 x_scales[:].bitcast(I32)[32 * q : 32 * q + 4, :],
                 xs_picked[:].bitcast(I32)[32 * q : 32 * q + 32 : 4, :],
             )
 
+        x_codes = []
+        for z in range(PASSES):
+            picked = sb.tile([P, J], U32, name="x_codes%d" % z, align_bytes=64)
+            nc.vector.tensor_copy(picked[:], xw_window[z][:].indirect(heads_list[:]))
+            x_codes.append(picked)
+
         w_codes, w_scales = [], []
         for z in range(PASSES):
-            w_bf = reused.tile([P, PACK, P, PACK], BF16, name="w_bf%d" % z, align_bytes=64, offset=bf_at + z * w_bytes // 2)
+            w_bf = reused.tile([P, PACK, P, PACK], BF16, name="w_bf%d" % z, align_bytes=64, offset=bf_at + (1 - z) * w_bytes // 2)
             src = w_raw[z][:].rearrange("p j (m t) -> p m j t", t=PACK)
             dst = w_bf[:].rearrange("p t m j -> p m j t")
-            nc.vector.tensor_copy(dst[:, :VECTOR_ROWS], src[:, :VECTOR_ROWS])
-            nc.scalar.activation(dst[:, VECTOR_ROWS:], src[:, VECTOR_ROWS:], ACT.Copy)
+            nc.vector.tensor_copy(dst[:, : VECTOR_ROWS[z]], src[:, : VECTOR_ROWS[z]])
+            nc.scalar.activation(dst[:, VECTOR_ROWS[z] :], src[:, VECTOR_ROWS[z] :], ACT.Copy)
             codes = sb.tile([P, R], U32, name="w_codes%d" % z, align_bytes=64)
             scales = sb.tile([P, R], U8, name="w_scales%d" % z, align_bytes=64)
             flat = w_bf[:].rearrange("p t m j -> p (t m j)")
@@ -92,23 +105,15 @@ def tile_list_headpicks_overtable_rowabove_kernel(tc, xt_words, xt_scales, w, tb
             w_scales.append(scales)
 
         tb_rows = tb.rearrange("(p t) v -> p t v", t=PACK)
-        tb_pair = reused.tile([P, 2, V], F32, name="tb_pair", align_bytes=64, offset=0)
+        tb_pair = reused.tile([P, 2, V], F32, name="tb_pair", align_bytes=64, offset=bf_at + w_bytes)
         nc.sync.dma_start(tb_pair[:], tb_rows[:, 0:2, :])
         tb_window = [tb_pair[:, 0, :], tb_pair[:, 1, :]]
         for t in range(2, PACK):
             tb_single = reused.tile([P, V], F32, name="tb_single%d" % t, align_bytes=64, offset=t * V * 4)
             nc.sync.dma_start(tb_single[:], tb_rows[:, t, :])
             tb_window.append(tb_single[:])
-        wb_codes = reused.tile([P, 2 * N], U8, name="wb_codes", align_bytes=64, offset=w_bytes)
-        nc.sync.dma_start(wb_codes[:].bitcast(I32), wb_words[0].bitcast(I32))
-        rs_sb = reused.tile([P, N], F32, name="rs_sb", align_bytes=64, offset=w_bytes + 2 * N)
+        rs_sb = reused.tile([P, N], F32, name="rs_sb", align_bytes=64, offset=0)
         nc.sync.dma_start(rs_sb[:], rs)
-
-        x_codes = []
-        for z in range(PASSES):
-            picked = sb.tile([P, J], U32, name="x_codes%d" % z, align_bytes=64)
-            nc.vector.tensor_copy(picked[:], xw_window[z][:].indirect(heads_list[:]))
-            x_codes.append(picked)
 
         acc = [ps.tile([P, J], F32, name="acc%d" % t) for t in range(PACK)]
         for z in range(PASSES):
@@ -123,46 +128,61 @@ def tile_list_headpicks_overtable_rowabove_kernel(tc, xt_words, xt_scales, w, tb
                     stop=(z == PASSES - 1),
                 )
 
-        gap = sb.tile([P, PACK, J], F32, name="gap", align_bytes=64)
-        for t in range(2):
-            tb_picked = sb.tile([P, J], F32, name="tb_picked%d" % t, align_bytes=64)
-            nc.scalar.activation(tb_picked[:], tb_window[t].indirect(table_list[:]), ACT.Copy)
-            nc.vector.tensor_tensor(gap[:, t, :], tb_picked[:], acc[t][:], ALU.subtract)
-        for t in range(2, PACK):
-            a_sb = sb.tile([P, J], F32, name="a_sb%d" % t, align_bytes=64)
-            nc.scalar.copy(a_sb[:], acc[t][:])
-            nc.vector.tensor_tensor(gap[:, t, :], tb_window[t].indirect(table_list[:]), a_sb[:], ALU.subtract)
-
-        hid = sb.tile([P, J, PACK], BF16, name="hid", align_bytes=64)
-        nc.vector.tensor_scalar(
-            hid[:].rearrange("p (c i) t -> p c t i", i=4),
-            gap[:].rearrange("p t (c i) -> p c t i", i=4),
-            -1.0, 0.0, ALU.mult, ALU.max,
-        )
+        half_j = J // 2
+        gap = sb.tile([P, 2, PACK, half_j], F32, name="gap", align_bytes=64)
+        tb_picked = [sb.tile([P, J], F32, name="tb_picked%d" % t, align_bytes=64) for t in range(PACK)]
+        for t in range(PACK):
+            if t == 1:
+                nc.vector.tensor_copy(tb_picked[t][:], tb_window[t].indirect(table_list[:]))
+            else:
+                nc.scalar.activation(tb_picked[t][:], tb_window[t].indirect(table_list[:]), ACT.Copy)
+        for t in range(PACK - 1):
+            nc.vector.tensor_tensor(
+                gap[:, :, t, :],
+                acc[t][:].rearrange("p (h j) -> p h j", h=2),
+                tb_picked[t][:].rearrange("p (h j) -> p h j", h=2),
+                ALU.subtract,
+            )
+        halves = [slice(h * half_j, (h + 1) * half_j) for h in range(2)]
+        for h in range(2):
+            nc.vector.tensor_tensor(
+                gap[:, h, PACK - 1, :], acc[PACK - 1][:, halves[h]], tb_picked[PACK - 1][:, halves[h]], ALU.subtract
+            )
+        hid = [sb.tile([P, half_j, PACK], BF16, name="hid%d" % h, align_bytes=64) for h in range(2)]
+        for h in range(2):
+            nc.vector.tensor_scalar(
+                hid[h][:].rearrange("p (c i) t -> p c t i", i=4),
+                gap[:, h].rearrange("p t (c i) -> p c t i", i=4),
+                0.0, None, ALU.max,
+            )
         h_codes = sb.tile([P, J], U32, name="h_codes", align_bytes=64)
         h_scales = sb.tile([P, J], U8, name="h_scales", align_bytes=64)
-        nc.vector.quantize_mx(
-            out=h_codes[:].bitcast(E5M2X4), scales=h_scales[:], in_=hid[:].rearrange("p j t -> p (j t)")
-        )
+        for h in range(2):
+            nc.vector.quantize_mx(
+                out=h_codes[:, halves[h]].bitcast(E5M2X4),
+                scales=h_scales[:, halves[h]],
+                in_=hid[h][:].rearrange("p j t -> p (j t)"),
+            )
 
-        prod = ps.tile([P, N], F32, name="prod")
-        nc.tensor.matmul_mx(
-            out=prod[:],
-            lhsT=h_codes[:].bitcast(E5M2X4),
-            lhsT_scale=h_scales[:],
-            rhs=wb_codes[:].bitcast(E2M1X4),
-            rhs_scale=wb_plane[:],
-            start=True,
-            stop=True,
-        )
+        prod = [ps.tile([P, N], F32, name="prod%d" % c) for c in range(2)]
+        for bank in prod:
+            nc.tensor.matmul_mx(
+                out=bank[:],
+                lhsT=h_codes[:].bitcast(E5M2X4),
+                lhsT_scale=h_scales[:],
+                rhs=wb_codes[:].bitcast(E2M1X4),
+                rhs_scale=wb_plane[:],
+                start=True,
+                stop=True,
+            )
 
         minus_rs = sb.tile([P, N], F32, name="minus_rs", align_bytes=64)
         nc.scalar.activation(minus_rs[:], rs_sb[:], ACT.Copy, scale=-0.3)
         shifted = sb.tile([P, N], F32, name="shifted", align_bytes=64)
-        nc.vector.tensor_tensor(shifted[:], prod[:], minus_rs[:], ALU.add)
+        nc.vector.tensor_tensor(shifted[:], prod[0][:], minus_rs[:], ALU.add)
         magnitude = sb.tile([P, N], F32, name="magnitude", align_bytes=64)
         mean = sb.tile([P, 1], F32, name="mean", align_bytes=64)
-        nc.scalar.activation(magnitude[:], prod[:], ACT.Abs, scale=1.0 / N, accum_out=mean[:])
+        nc.scalar.activation(magnitude[:], prod[1][:], ACT.Abs, scale=1.0 / N, accum_out=mean[:])
         result = sb.tile([P, N], F32, name="result", align_bytes=64)
         nc.vector.scalar_tensor_tensor(result[:], shifted[:], mean[:], minus_rs[:], ALU.subtract, ALU.max)
         nc.sync.dma_start(out, result[:])

@@ -34,6 +34,7 @@ def tile_list_headpicks_overtable_rowabove_kernel(tc, xt_words, xt_scales, w, tb
         table_list = sb.tile([P, J // 16], U16, name="table_list")
         xs_picked = sb.tile([P, J], U8, name="xs_picked", align_bytes=64)
         x_scales = sb.tile([P, PASSES * J], U8, name="x_scales", align_bytes=64)
+        wb_rows = sb.tile([P, N], U8, name="wb_rows", align_bytes=64)
         wb_plane = sb.tile([P, N], U8, name="wb_plane", align_bytes=64)
         w_bytes = PACK * R * 4
         w_raw = [
@@ -45,7 +46,7 @@ def tile_list_headpicks_overtable_rowabove_kernel(tc, xt_words, xt_scales, w, tb
 
         nc.vector.memset(xs_window[:].bitcast(I32), 0)
         nc.gpsimd.memset(x_scales[:].bitcast(I32), 0)
-        nc.gpsimd.memset(wb_plane[:].bitcast(I32), 0)
+        nc.gpsimd.memset(wb_rows[:].bitcast(I32), 0)
 
         nc.sync.dma_start(heads_list[:], offs)
         nc.scalar.dma_start(
@@ -63,9 +64,10 @@ def tile_list_headpicks_overtable_rowabove_kernel(tc, xt_words, xt_scales, w, tb
         nc.sync.dma_start(xw_window[1][:].bitcast(I32), x_rows[1])
         for q in range(QUADS):
             nc.gpsimd.dma_start(
-                wb_plane[:].bitcast(I32)[32 * q : 32 * q + 4, :],
+                wb_rows[:].bitcast(I32)[32 * q : 32 * q + 4, :],
                 wb_scales[0, 4 * q : 4 * q + 4, :].bitcast(I32),
             )
+        nc.gpsimd.tensor_copy(wb_plane[:].bitcast(I32), wb_rows[:].bitcast(I32))
 
         warm_in = sb.tile([P, 1], F32, name="warm_in")
         warm_out = sb.tile([P, 1], F32, name="warm_out")
@@ -116,8 +118,8 @@ def tile_list_headpicks_overtable_rowabove_kernel(tc, xt_words, xt_scales, w, tb
         nc.sync.dma_start(rs_sb[:], rs)
 
         acc = [ps.tile([P, J], F32, name="acc%d" % t) for t in range(PACK)]
-        for z in range(PASSES):
-            for t in range(PACK):
+        for t in range(PACK):
+            for z in range(PASSES):
                 nc.tensor.matmul_mx(
                     out=acc[t][:],
                     lhsT=w_codes[z][:, P * t : P * (t + 1)].bitcast(E5M2X4),
@@ -164,25 +166,30 @@ def tile_list_headpicks_overtable_rowabove_kernel(tc, xt_words, xt_scales, w, tb
                 in_=hid[h][:].rearrange("p j t -> p (j t)"),
             )
 
-        prod = [ps.tile([P, N], F32, name="prod%d" % c) for c in range(2)]
-        for bank in prod:
+        half_n = N // 2
+        cols = [slice(c * half_n, (c + 1) * half_n) for c in range(2)]
+        whole = ps.tile([P, N], F32, name="whole")
+        parts = [ps.tile([P, half_n], F32, name="part%d" % c) for c in range(2)]
+        for bank, span in [(whole, slice(0, N))] + list(zip(parts, cols)):
             nc.tensor.matmul_mx(
                 out=bank[:],
                 lhsT=h_codes[:].bitcast(E5M2X4),
                 lhsT_scale=h_scales[:],
-                rhs=wb_codes[:].bitcast(E2M1X4),
-                rhs_scale=wb_plane[:],
+                rhs=wb_codes[:, 2 * span.start : 2 * span.stop].bitcast(E2M1X4),
+                rhs_scale=wb_plane[:, span],
                 start=True,
                 stop=True,
             )
 
         minus_rs = sb.tile([P, N], F32, name="minus_rs", align_bytes=64)
-        nc.scalar.activation(minus_rs[:], rs_sb[:], ACT.Copy, scale=-0.3)
-        shifted = sb.tile([P, N], F32, name="shifted", align_bytes=64)
-        nc.vector.tensor_tensor(shifted[:], prod[0][:], minus_rs[:], ALU.add)
+        nc.vector.tensor_scalar(minus_rs[:], rs_sb[:], -0.3, None, ALU.mult)
         magnitude = sb.tile([P, N], F32, name="magnitude", align_bytes=64)
         mean = sb.tile([P, 1], F32, name="mean", align_bytes=64)
-        nc.scalar.activation(magnitude[:], prod[1][:], ACT.Abs, scale=1.0 / N, accum_out=mean[:])
-        result = sb.tile([P, N], F32, name="result", align_bytes=64)
-        nc.vector.scalar_tensor_tensor(result[:], shifted[:], mean[:], minus_rs[:], ALU.subtract, ALU.max)
-        nc.sync.dma_start(out, result[:])
+        nc.scalar.activation(magnitude[:], whole[:], ACT.Abs, scale=1.0 / N, accum_out=mean[:])
+        shifted = [sb.tile([P, half_n], F32, name="shifted%d" % c, align_bytes=64) for c in range(2)]
+        result = [sb.tile([P, half_n], F32, name="result%d" % c, align_bytes=64) for c in range(2)]
+        for c in range(2):
+            nc.vector.tensor_tensor(shifted[c][:], parts[c][:], minus_rs[:, cols[c]], ALU.add)
+        for c, queue in enumerate((nc.scalar, nc.sync)):
+            nc.vector.scalar_tensor_tensor(result[c][:], shifted[c][:], mean[:], minus_rs[:, cols[c]], ALU.subtract, ALU.max)
+            queue.dma_start(out[:, cols[c]], result[c][:])

@@ -19,7 +19,7 @@ PACK = 4
 K, T, J, R, V, N = 1024, 512, 128, 512, 512, 256
 PASSES = K // (P * PACK)
 QUADS = 4
-VECTOR_ROWS = (84, 64)
+VECTOR_ROWS = (72, 64)
 FLOPS = 2 * K * R * J + 2 * R * J * N
 
 
@@ -41,20 +41,20 @@ def tile_list_headpicks_overtable_rowabove_kernel(tc, xt_words, xt_scales, w, tb
             reused.tile([P, PACK, R], F32, name="w_raw%d" % z, align_bytes=64, offset=z * w_bytes) for z in range(PASSES)
         ]
         bf_at = PASSES * w_bytes
-        xs_window = reused.tile([P, T], U8, name="xs_window", align_bytes=64, offset=bf_at + w_bytes - 256)
+        xs_window = reused.tile([P, T], U8, name="xs_window", align_bytes=64, offset=bf_at + 2 * 4 * R - 256)
         xw_window = [sb.tile([P, T], U32, name="xw_window%d" % z, align_bytes=64) for z in range(PASSES)]
 
         nc.vector.memset(xs_window[:].bitcast(I32), 0)
         nc.gpsimd.memset(x_scales[:].bitcast(I32), 0)
         nc.gpsimd.memset(wb_rows[:].bitcast(I32), 0)
 
-        nc.sync.dma_start(heads_list[:], offs)
         nc.scalar.dma_start(
             xs_window[:].bitcast(I32)[0:P:4, :],
             xt_scales.rearrange("z q c -> q z c").bitcast(I32),
         )
         w_rows = w.rearrange("(z p j) r -> z p j r", z=PASSES, j=PACK)
         nc.sync.dma_start(w_raw[0][:], w_rows[0])
+        nc.sync.dma_start(heads_list[:], offs)
         nc.sync.dma_start(table_list[:], offs2)
         wb_codes = sb.tile([P, 2 * N], U8, name="wb_codes", align_bytes=64)
         nc.sync.dma_start(wb_codes[:].bitcast(I32), wb_words[0].bitcast(I32))
@@ -89,12 +89,12 @@ def tile_list_headpicks_overtable_rowabove_kernel(tc, xt_words, xt_scales, w, tb
 
         w_codes, w_scales = [], []
         for z in range(PASSES):
-            w_bf = reused.tile([P, PACK, P, PACK], BF16, name="w_bf%d" % z, align_bytes=64, offset=bf_at + (1 - z) * w_bytes // 2)
+            w_bf = sb.tile([P, PACK, P, PACK], BF16, name="w_bf%d" % z, align_bytes=64)
             src = w_raw[z][:].rearrange("p j (m t) -> p m j t", t=PACK)
             dst = w_bf[:].rearrange("p t m j -> p m j t")
             nc.vector.tensor_copy(dst[:, : VECTOR_ROWS[z]], src[:, : VECTOR_ROWS[z]])
             nc.scalar.activation(dst[:, VECTOR_ROWS[z] :], src[:, VECTOR_ROWS[z] :], ACT.Copy)
-            codes = sb.tile([P, R], U32, name="w_codes%d" % z, align_bytes=64)
+            codes = reused.tile([P, R], U32, name="w_codes%d" % z, align_bytes=64, offset=bf_at + (1 - z) * 4 * R)
             scales = sb.tile([P, R], U8, name="w_scales%d" % z, align_bytes=64)
             flat = w_bf[:].rearrange("p t m j -> p (t m j)")
             for half in range(2):
@@ -107,7 +107,7 @@ def tile_list_headpicks_overtable_rowabove_kernel(tc, xt_words, xt_scales, w, tb
             w_scales.append(scales)
 
         tb_rows = tb.rearrange("(p t) v -> p t v", t=PACK)
-        tb_pair = reused.tile([P, 2, V], F32, name="tb_pair", align_bytes=64, offset=bf_at + w_bytes)
+        tb_pair = reused.tile([P, 2, V], F32, name="tb_pair", align_bytes=64, offset=bf_at + 2 * 4 * R)
         nc.sync.dma_start(tb_pair[:], tb_rows[:, 0:2, :])
         tb_window = [tb_pair[:, 0, :], tb_pair[:, 1, :]]
         for t in range(2, PACK):

from contextlib import ExitStack

import concourse.mybir as mybir

F32 = mybir.dt.float32
BF16 = mybir.dt.bfloat16
I32 = mybir.dt.int32
U32 = mybir.dt.uint32
U16 = mybir.dt.uint16
U8 = mybir.dt.uint8
E4M3X4 = mybir.dt.float8_e4m3fn_x4
E5M2X4 = mybir.dt.float8_e5m2_x4
E2M1X4 = mybir.dt.float4_e2m1fn_x4
ALU = mybir.AluOpType
ACT = mybir.ActivationFunctionType

P = 128
PACK = 4
K, T, J, R, V, N = 1024, 512, 128, 512, 512, 256
PASSES = K // (P * PACK)
QUADS = 4
VECTOR_ROWS = (72, 64)
FLOPS = 2 * K * R * J + 2 * R * J * N


def tile_list_headpicks_overtable_rowabove_kernel(tc, xt_words, xt_scales, w, tb, wb_words, wb_scales, rs, offs, offs2, out):
    nc = tc.nc
    with ExitStack() as ctx:
        sb = ctx.enter_context(tc.tile_pool(name="sb", bufs=1))
        reused = ctx.enter_context(tc.tile_pool(name="reused", bufs=1))
        ps = ctx.enter_context(tc.psum_pool(name="ps", bufs=1))

        heads_list = sb.tile([P, J // 16], U16, name="heads_list")
        table_list = sb.tile([P, J // 16], U16, name="table_list")
        xs_picked = sb.tile([P, J], U8, name="xs_picked", align_bytes=64)
        x_scales = sb.tile([P, PASSES * J], U8, name="x_scales", align_bytes=64)
        wb_rows = sb.tile([P, N], U8, name="wb_rows", align_bytes=64)
        wb_plane = sb.tile([P, N], U8, name="wb_plane", align_bytes=64)
        w_bytes = PACK * R * 4
        w_raw = [
            reused.tile([P, PACK, R], F32, name="w_raw%d" % z, align_bytes=64, offset=z * w_bytes) for z in range(PASSES)
        ]
        bf_at = PASSES * w_bytes
        xs_window = reused.tile([P, T], U8, name="xs_window", align_bytes=64, offset=bf_at + 2 * 4 * R - 256)
        xw_window = [sb.tile([P, T], U32, name="xw_window%d" % z, align_bytes=64) for z in range(PASSES)]

        nc.vector.memset(xs_window[:].bitcast(I32), 0)
        nc.gpsimd.memset(x_scales[:].bitcast(I32), 0)
        nc.gpsimd.memset(wb_rows[:].bitcast(I32), 0)

        nc.scalar.dma_start(
            xs_window[:].bitcast(I32)[0:P:4, :],
            xt_scales.rearrange("z q c -> q z c").bitcast(I32),
        )
        w_rows = w.rearrange("(z p j) r -> z p j r", z=PASSES, j=PACK)
        nc.sync.dma_start(w_raw[0][:], w_rows[0])
        nc.sync.dma_start(heads_list[:], offs)
        nc.sync.dma_start(table_list[:], offs2)
        wb_codes = sb.tile([P, 2 * N], U8, name="wb_codes", align_bytes=64)
        nc.sync.dma_start(wb_codes[:].bitcast(I32), wb_words[0].bitcast(I32))
        x_rows = xt_words.rearrange("z p c b -> z p (c b)").bitcast(I32)
        nc.sync.dma_start(w_raw[1][:], w_rows[1])
        nc.sync.dma_start(xw_window[0][:].bitcast(I32), x_rows[0])
        nc.sync.dma_start(xw_window[1][:].bitcast(I32), x_rows[1])
        for q in range(QUADS):
            nc.gpsimd.dma_start(
                wb_rows[:].bitcast(I32)[32 * q : 32 * q + 4, :],
                wb_scales[0, 4 * q : 4 * q + 4, :].bitcast(I32),
            )
        nc.gpsimd.tensor_copy(wb_plane[:].bitcast(I32), wb_rows[:].bitcast(I32))

        warm_in = sb.tile([P, 1], F32, name="warm_in")
        warm_out = sb.tile([P, 1], F32, name="warm_out")
        nc.vector.memset(warm_in[:], 0.0)
        nc.scalar.activation(warm_out[:], warm_in[:], ACT.Abs)

        nc.vector.tensor_copy(xs_picked[:], xs_window[:].indirect(heads_list[:]))
        for q in range(QUADS):
            nc.sync.dma_start(
                x_scales[:].bitcast(I32)[32 * q : 32 * q + 4, :],
                xs_picked[:].bitcast(I32)[32 * q : 32 * q + 32 : 4, :],
            )

        x_codes = []
        for z in range(PASSES):
            picked = sb.tile([P, J], U32, name="x_codes%d" % z, align_bytes=64)
            nc.vector.tensor_copy(picked[:], xw_window[z][:].indirect(heads_list[:]))
            x_codes.append(picked)

        w_codes, w_scales = [], []
        for z in range(PASSES):
            w_bf = sb.tile([P, PACK, P, PACK], BF16, name="w_bf%d" % z, align_bytes=64)
            src = w_raw[z][:].rearrange("p j (m t) -> p m j t", t=PACK)
            dst = w_bf[:].rearrange("p t m j -> p m j t")
            nc.vector.tensor_copy(dst[:, : VECTOR_ROWS[z]], src[:, : VECTOR_ROWS[z]])
            nc.scalar.activation(dst[:, VECTOR_ROWS[z] :], src[:, VECTOR_ROWS[z] :], ACT.Copy)
            codes = reused.tile([P, R], U32, name="w_codes%d" % z, align_bytes=64, offset=bf_at + (1 - z) * 4 * R)
            scales = sb.tile([P, R], U8, name="w_scales%d" % z, align_bytes=64)
            flat = w_bf[:].rearrange("p t m j -> p (t m j)")
            for half in range(2):
                nc.vector.quantize_mx(
                    out=codes[:, 256 * half : 256 * (half + 1)].bitcast(E5M2X4),
                    scales=scales[:, 256 * half : 256 * (half + 1)],
                    in_=flat[:, 1024 * half : 1024 * (half + 1)],
                )
            w_codes.append(codes)
            w_scales.append(scales)

        tb_rows = tb.rearrange("(p t) v -> p t v", t=PACK)
        tb_pair = reused.tile([P, 2, V], F32, name="tb_pair", align_bytes=64, offset=bf_at + 2 * 4 * R)
        nc.sync.dma_start(tb_pair[:], tb_rows[:, 0:2, :])
        tb_window = [tb_pair[:, 0, :], tb_pair[:, 1, :]]
        for t in range(2, PACK):
            tb_single = reused.tile([P, V], F32, name="tb_single%d" % t, align_bytes=64, offset=t * V * 4)
            nc.sync.dma_start(tb_single[:], tb_rows[:, t, :])
            tb_window.append(tb_single[:])
        rs_sb = reused.tile([P, N], F32, name="rs_sb", align_bytes=64, offset=0)
        nc.sync.dma_start(rs_sb[:], rs)

        acc = [ps.tile([P, J], F32, name="acc%d" % t) for t in range(PACK)]
        for t in range(PACK):
            for z in range(PASSES):
                nc.tensor.matmul_mx(
                    out=acc[t][:],
                    lhsT=w_codes[z][:, P * t : P * (t + 1)].bitcast(E5M2X4),
                    lhsT_scale=w_scales[z][:, P * t : P * (t + 1)],
                    rhs=x_codes[z][:].bitcast(E4M3X4),
                    rhs_scale=x_scales[:, J * z : J * (z + 1)],
                    start=(z == 0),
                    stop=(z == PASSES - 1),
                )

        half_j = J // 2
        gap = sb.tile([P, 2, PACK, half_j], F32, name="gap", align_bytes=64)
        tb_picked = [sb.tile([P, J], F32, name="tb_picked%d" % t, align_bytes=64) for t in range(PACK)]
        for t in range(PACK):
            if t == 1:
                nc.vector.tensor_copy(tb_picked[t][:], tb_window[t].indirect(table_list[:]))
            else:
                nc.scalar.activation(tb_picked[t][:], tb_window[t].indirect(table_list[:]), ACT.Copy)
        for t in range(PACK - 1):
            nc.vector.tensor_tensor(
                gap[:, :, t, :],
                acc[t][:].rearrange("p (h j) -> p h j", h=2),
                tb_picked[t][:].rearrange("p (h j) -> p h j", h=2),
                ALU.subtract,
            )
        halves = [slice(h * half_j, (h + 1) * half_j) for h in range(2)]
        for h in range(2):
            nc.vector.tensor_tensor(
                gap[:, h, PACK - 1, :], acc[PACK - 1][:, halves[h]], tb_picked[PACK - 1][:, halves[h]], ALU.subtract
            )
        hid = [sb.tile([P, half_j, PACK], BF16, name="hid%d" % h, align_bytes=64) for h in range(2)]
        for h in range(2):
            nc.vector.tensor_scalar(
                hid[h][:].rearrange("p (c i) t -> p c t i", i=4),
                gap[:, h].rearrange("p t (c i) -> p c t i", i=4),
                0.0, None, ALU.max,
            )
        h_codes = sb.tile([P, J], U32, name="h_codes", align_bytes=64)
        h_scales = sb.tile([P, J], U8, name="h_scales", align_bytes=64)
        for h in range(2):
            nc.vector.quantize_mx(
                out=h_codes[:, halves[h]].bitcast(E5M2X4),
                scales=h_scales[:, halves[h]],
                in_=hid[h][:].rearrange("p j t -> p (j t)"),
            )

        half_n = N // 2
        cols = [slice(c * half_n, (c + 1) * half_n) for c in range(2)]
        whole = ps.tile([P, N], F32, name="whole")
        parts = [ps.tile([P, half_n], F32, name="part%d" % c) for c in range(2)]
        for bank, span in [(whole, slice(0, N))] + list(zip(parts, cols)):
            nc.tensor.matmul_mx(
                out=bank[:],
                lhsT=h_codes[:].bitcast(E5M2X4),
                lhsT_scale=h_scales[:],
                rhs=wb_codes[:, 2 * span.start : 2 * span.stop].bitcast(E2M1X4),
                rhs_scale=wb_plane[:, span],
                start=True,
                stop=True,
            )

        minus_rs = sb.tile([P, N], F32, name="minus_rs", align_bytes=64)
        nc.vector.tensor_scalar(minus_rs[:], rs_sb[:], -0.3, None, ALU.mult)
        magnitude = sb.tile([P, N], F32, name="magnitude", align_bytes=64)
        mean = sb.tile([P, 1], F32, name="mean", align_bytes=64)
        nc.scalar.activation(magnitude[:], whole[:], ACT.Abs, scale=1.0 / N, accum_out=mean[:])
        shifted = [sb.tile([P, half_n], F32, name="shifted%d" % c, align_bytes=64) for c in range(2)]
        result = [sb.tile([P, half_n], F32, name="result%d" % c, align_bytes=64) for c in range(2)]
        for c in range(2):
            nc.vector.tensor_tensor(shifted[c][:], parts[c][:], minus_rs[:, cols[c]], ALU.add)
        for c, queue in enumerate((nc.scalar, nc.sync)):
            nc.vector.scalar_tensor_tensor(result[c][:], shifted[c][:], mean[:], minus_rs[:, cols[c]], ALU.subtract, ALU.max)
            queue.dma_start(out[:, cols[c]], result[c][:])
